import numpy as np
import ml_dtypes

BF16 = ml_dtypes.bfloat16


def bf(x):
    return np.asarray(x, np.float32).astype(BF16)


def f32(x):
    return np.asarray(x, np.float32)


def f64(x):
    return np.asarray(x).astype(np.float64)


def striped(idx):
    return np.tile(idx.reshape(-1, 16).T, (8, 1))


def rows(idx, k):
    return np.tile(idx, (k, 1))


def look(tab, idx):
    return np.take_along_axis(f64(tab), rows(idx, len(tab)), axis=1)


K, S, D, V, N, M = 256, 256, 2, 64, 128, 512


def setup_inputs():
    return {"tab": f32(np.random.standard_normal((K, S))), "th": f32(np.random.standard_normal((K, V))), "w": bf(np.random.standard_normal((K, M)) / np.sqrt(K)), "b": f32(0.5 * np.random.standard_normal((M, 1))), "offs": striped(np.random.permutation(S)[:N])}


def reference(tab, th, w, b, offs):
    idx = offs[:16].T.reshape(-1)
    x = sum((look(tab, idx[d * V:(d + 1) * V]) >= f64(th)) * 1.0 for d in range(D)) / D
    y = f64(w).T @ x
    return np.maximum(y + f64(b), 0.0)

@@ -1,0 +1,51 @@
+import concourse.mybir as mybir
+
+F32, BF16, U16 = mybir.dt.float32, mybir.dt.bfloat16, mybir.dt.uint16
+ALU = mybir.AluOpType
+RELU = mybir.ActivationFunctionType.Relu
+
+P = 128
+K, S, D, V, M = 256, 256, 2, 64, 512
+ROW_BLOCKS = K // P
+OUT_BLOCKS = M // P
+LIST_COLS = V // 16
+FLOPS = 2 * K * M * V
+
+
+def tile_lookup_vote_ge_relu_kernel(tc, tab, th, w, b, offs, out):
+    nc = tc.nc
+    tab_blocks = tab.rearrange("(p k) s -> k p s", k=ROW_BLOCKS)
+    with (
+        tc.tile_pool(name="held", bufs=1) as held,
+        tc.psum_pool(name="psum", bufs=1) as psum,
+    ):
+        offsets = held.tile([P, D * LIST_COLS], U16, name="offsets")
+        nc.sync.dma_start(offsets[:], offs)
+        windows = [held.tile([P, S], F32, name=f"window{k}") for k in range(ROW_BLOCKS)]
+        for k in range(ROW_BLOCKS):
+            nc.sync.dma_start(windows[k][:], tab_blocks[k])
+        thresholds = held.tile([P, ROW_BLOCKS, V], F32, name="thresholds")
+        nc.scalar.dma_start(thresholds[:], th.rearrange("(p k) j -> p k j", k=ROW_BLOCKS))
+        weights = held.tile([P, ROW_BLOCKS, M], BF16, name="weights")
+        nc.scalar.dma_start(weights[:], w.rearrange("(p k) m -> p k m", k=ROW_BLOCKS))
+        bias = held.tile([P, OUT_BLOCKS], F32, name="bias")
+        nc.scalar.dma_start(bias[:], b.rearrange("(p c) one -> p (c one)", c=OUT_BLOCKS))
+
+        counts = []
+        for k in range(ROW_BLOCKS):
+            votes = held.tile([P, D, V], F32, name=f"votes{k}")
+            for d in range(D):
+                picked = windows[k][:].indirect(offsets[:, d * LIST_COLS:(d + 1) * LIST_COLS])
+                nc.vector.tensor_tensor(votes[:, d, :], picked, thresholds[:, k, :], ALU.is_ge)
+            count = held.tile([P, V], BF16, name=f"count{k}")
+            nc.vector.tensor_tensor(count[:], votes[:, 0, :], votes[:, 1, :], ALU.add)
+            counts.append(count)
+
+        result = held.tile([P, OUT_BLOCKS, V], F32, name="result")
+        for c in range(OUT_BLOCKS):
+            acc = psum.tile([P, V], F32, name=f"acc{c}")
+            for k in range(ROW_BLOCKS):
+                nc.tensor.matmul(acc[:], weights[:, k, c::OUT_BLOCKS], counts[k][:],
+                                 start=(k == 0), stop=(k == ROW_BLOCKS - 1))
+            nc.scalar.activation(result[:, c, :], acc[:], RELU, bias=bias[:, c:c + 1], scale=1.0 / D)
+        nc.sync.dma_start(out.rearrange("(p c) j -> p c j", c=OUT_BLOCKS), result[:])

@@ -20,18 +20,23 @@ def tile_lookup_vote_ge_relu_kernel(tc, tab, th, w, b, offs, out):
         tc.psum_pool(name="psum", bufs=1) as psum,
     ):
         offsets = held.tile([P, D * LIST_COLS], U16, name="offsets")
-        nc.sync.dma_start(offsets[:], offs)
         windows = [held.tile([P, S], F32, name=f"window{k}") for k in range(ROW_BLOCKS)]
-        for k in range(ROW_BLOCKS):
-            nc.sync.dma_start(windows[k][:], tab_blocks[k])
         thresholds = held.tile([P, ROW_BLOCKS, V], F32, name="thresholds")
-        nc.scalar.dma_start(thresholds[:], th.rearrange("(p k) j -> p k j", k=ROW_BLOCKS))
         weights = held.tile([P, ROW_BLOCKS, M], BF16, name="weights")
-        nc.scalar.dma_start(weights[:], w.rearrange("(p k) m -> p k m", k=ROW_BLOCKS))
         bias = held.tile([P, OUT_BLOCKS], F32, name="bias")
+        nc.sync.dma_start(offsets[:], offs)
+        nc.scalar.dma_start(windows[0][:], tab_blocks[0])
+        nc.sync.dma_start(thresholds[:], th.rearrange("(p k) j -> p k j", k=ROW_BLOCKS))
+        nc.sync.dma_start(windows[1][:], tab_blocks[1])
+        nc.sync.dma_start(weights[:], w.rearrange("(p k) m -> p k m", k=ROW_BLOCKS))
         nc.scalar.dma_start(bias[:], b.rearrange("(p c) one -> p (c one)", c=OUT_BLOCKS))
 
-        counts = []
+        warm_in = held.tile([P, 1], F32, name="warm_in")
+        warm_out = held.tile([P, 1], F32, name="warm_out")
+        nc.vector.memset(warm_in[:], 0.0)
+        nc.scalar.activation(warm_out[:], warm_in[:], RELU)
+
+        accs = [psum.tile([P, V], F32, name=f"acc{c}") for c in range(OUT_BLOCKS)]
         for k in range(ROW_BLOCKS):
             votes = held.tile([P, D, V], F32, name=f"votes{k}")
             for d in range(D):
@@ -39,13 +44,11 @@ def tile_lookup_vote_ge_relu_kernel(tc, tab, th, w, b, offs, out):
                 nc.vector.tensor_tensor(votes[:, d, :], picked, thresholds[:, k, :], ALU.is_ge)
             count = held.tile([P, V], BF16, name=f"count{k}")
             nc.vector.tensor_tensor(count[:], votes[:, 0, :], votes[:, 1, :], ALU.add)
-            counts.append(count)
+            for c in range(OUT_BLOCKS):
+                nc.tensor.matmul(accs[c][:], weights[:, k, c::OUT_BLOCKS], count[:],
+                                 start=(k == 0), stop=(k == ROW_BLOCKS - 1))
 
         result = held.tile([P, OUT_BLOCKS, V], F32, name="result")
         for c in range(OUT_BLOCKS):
-            acc = psum.tile([P, V], F32, name=f"acc{c}")
-            for k in range(ROW_BLOCKS):
-                nc.tensor.matmul(acc[:], weights[:, k, c::OUT_BLOCKS], counts[k][:],
-                                 start=(k == 0), stop=(k == ROW_BLOCKS - 1))
-            nc.scalar.activation(result[:, c, :], acc[:], RELU, bias=bias[:, c:c + 1], scale=1.0 / D)
+            nc.scalar.activation(result[:, c, :], accs[c][:], RELU, bias=bias[:, c:c + 1], scale=1.0 / D)
         nc.sync.dma_start(out.rearrange("(p c) j -> p c j", c=OUT_BLOCKS), result[:])

@@ -36,19 +36,19 @@ def tile_lookup_vote_ge_relu_kernel(tc, tab, th, w, b, offs, out):
         nc.vector.memset(warm_in[:], 0.0)
         nc.scalar.activation(warm_out[:], warm_in[:], RELU)
 
-        accs = [psum.tile([P, V], F32, name=f"acc{c}") for c in range(OUT_BLOCKS)]
+        votes = held.tile([P, D, ROW_BLOCKS, V], F32, name="votes")
         for k in range(ROW_BLOCKS):
-            votes = held.tile([P, D, V], F32, name=f"votes{k}")
             for d in range(D):
                 picked = windows[k][:].indirect(offsets[:, d * LIST_COLS:(d + 1) * LIST_COLS])
-                nc.vector.tensor_tensor(votes[:, d, :], picked, thresholds[:, k, :], ALU.is_ge)
-            count = held.tile([P, V], BF16, name=f"count{k}")
-            nc.vector.tensor_tensor(count[:], votes[:, 0, :], votes[:, 1, :], ALU.add)
-            for c in range(OUT_BLOCKS):
-                nc.tensor.matmul(accs[c][:], weights[:, k, c::OUT_BLOCKS], count[:],
-                                 start=(k == 0), stop=(k == ROW_BLOCKS - 1))
+                nc.vector.tensor_tensor(votes[:, d, k, :], picked, thresholds[:, k, :], ALU.is_ge)
+        counts = held.tile([P, ROW_BLOCKS, V], BF16, name="counts")
+        nc.vector.tensor_tensor(counts[:], votes[:, 0], votes[:, 1], ALU.add)
 
         result = held.tile([P, OUT_BLOCKS, V], F32, name="result")
         for c in range(OUT_BLOCKS):
-            nc.scalar.activation(result[:, c, :], accs[c][:], RELU, bias=bias[:, c:c + 1], scale=1.0 / D)
+            acc = psum.tile([P, V], F32, name=f"acc{c}")
+            for k in range(ROW_BLOCKS):
+                nc.tensor.matmul(acc[:], weights[:, k, c::OUT_BLOCKS], counts[:, k, :],
+                                 start=(k == 0), stop=(k == ROW_BLOCKS - 1))
+            nc.scalar.activation(result[:, c, :], acc[:], RELU, bias=bias[:, c:c + 1], scale=1.0 / D)
         nc.sync.dma_start(out.rearrange("(p c) j -> p c j", c=OUT_BLOCKS), result[:])

@@ -9,6 +9,7 @@ K, S, D, V, M = 256, 256, 2, 64, 512
 ROW_BLOCKS = K // P
 OUT_BLOCKS = M // P
 LIST_COLS = V // 16
+WARM_COLS, WARM_MATMULS = 512, 4
 FLOPS = 2 * K * M * V
 
 
@@ -35,6 +36,11 @@ def tile_lookup_vote_ge_relu_kernel(tc, tab, th, w, b, offs, out):
         warm_out = held.tile([P, 1], F32, name="warm_out")
         nc.vector.memset(warm_in[:], 0.0)
         nc.scalar.activation(warm_out[:], warm_in[:], RELU)
+        zeros = held.tile([P, WARM_COLS], BF16, name="zeros")
+        warm_acc = psum.tile([P, WARM_COLS], F32, name="warm_acc")
+        nc.vector.memset(zeros[:], 0.0)
+        for i in range(WARM_MATMULS):
+            nc.tensor.matmul(warm_acc[:], zeros[:, :P], zeros[:], start=True, stop=True)
 
         votes = held.tile([P, D, ROW_BLOCKS, V], F32, name="votes")
         for k in range(ROW_BLOCKS):

import concourse.mybir as mybir

F32, BF16, U16 = mybir.dt.float32, mybir.dt.bfloat16, mybir.dt.uint16
ALU = mybir.AluOpType
RELU = mybir.ActivationFunctionType.Relu

P = 128
K, S, D, V, M = 256, 256, 2, 64, 512
ROW_BLOCKS = K // P
OUT_BLOCKS = M // P
LIST_COLS = V // 16
WARM_COLS, WARM_MATMULS = 512, 4
FLOPS = 2 * K * M * V


def tile_lookup_vote_ge_relu_kernel(tc, tab, th, w, b, offs, out):
    nc = tc.nc
    tab_blocks = tab.rearrange("(p k) s -> k p s", k=ROW_BLOCKS)
    with (
        tc.tile_pool(name="held", bufs=1) as held,
        tc.psum_pool(name="psum", bufs=1) as psum,
    ):
        offsets = held.tile([P, D * LIST_COLS], U16, name="offsets")
        windows = [held.tile([P, S], F32, name=f"window{k}") for k in range(ROW_BLOCKS)]
        thresholds = held.tile([P, ROW_BLOCKS, V], F32, name="thresholds")
        weights = held.tile([P, ROW_BLOCKS, M], BF16, name="weights")
        bias = held.tile([P, OUT_BLOCKS], F32, name="bias")
        nc.sync.dma_start(offsets[:], offs)
        nc.scalar.dma_start(windows[0][:], tab_blocks[0])
        nc.sync.dma_start(thresholds[:], th.rearrange("(p k) j -> p k j", k=ROW_BLOCKS))
        nc.sync.dma_start(windows[1][:], tab_blocks[1])
        nc.sync.dma_start(weights[:], w.rearrange("(p k) m -> p k m", k=ROW_BLOCKS))
        nc.scalar.dma_start(bias[:], b.rearrange("(p c) one -> p (c one)", c=OUT_BLOCKS))

        warm_in = held.tile([P, 1], F32, name="warm_in")
        warm_out = held.tile([P, 1], F32, name="warm_out")
        nc.vector.memset(warm_in[:], 0.0)
        nc.scalar.activation(warm_out[:], warm_in[:], RELU)
        zeros = held.tile([P, WARM_COLS], BF16, name="zeros")
        warm_acc = psum.tile([P, WARM_COLS], F32, name="warm_acc")
        nc.vector.memset(zeros[:], 0.0)
        for i in range(WARM_MATMULS):
            nc.tensor.matmul(warm_acc[:], zeros[:, :P], zeros[:], start=True, stop=True)

        votes = held.tile([P, D, ROW_BLOCKS, V], F32, name="votes")
        for k in range(ROW_BLOCKS):
            for d in range(D):
                picked = windows[k][:].indirect(offsets[:, d * LIST_COLS:(d + 1) * LIST_COLS])
                nc.vector.tensor_tensor(votes[:, d, k, :], picked, thresholds[:, k, :], ALU.is_ge)
        counts = held.tile([P, ROW_BLOCKS, V], BF16, name="counts")
        nc.vector.tensor_tensor(counts[:], votes[:, 0], votes[:, 1], ALU.add)

        result = held.tile([P, OUT_BLOCKS, V], F32, name="result")
        for c in range(OUT_BLOCKS):
            acc = psum.tile([P, V], F32, name=f"acc{c}")
            for k in range(ROW_BLOCKS):
                nc.tensor.matmul(acc[:], weights[:, k, c::OUT_BLOCKS], counts[:, k, :],
                                 start=(k == 0), stop=(k == ROW_BLOCKS - 1))
            nc.scalar.activation(result[:, c, :], acc[:], RELU, bias=bias[:, c:c + 1], scale=1.0 / D)
        nc.sync.dma_start(out.rearrange("(p c) j -> p c j", c=OUT_BLOCKS), result[:])
